import numpy as np
import ml_dtypes


def mxq(x, axis, fmt="e4m3"):
    dtype, down = {"e4m3": (ml_dtypes.float8_e4m3fn, 7), "e5m2": (ml_dtypes.float8_e5m2, 14)}[fmt]
    v = np.moveaxis(np.asarray(x, np.float32).astype(ml_dtypes.bfloat16).astype(np.float64), axis, -1)
    blocks = v.reshape(v.shape[:-1] + (-1, 32))
    amax = np.abs(blocks).max(-1, keepdims=True)
    byte = np.maximum(np.where(amax > 0, np.frexp(amax)[1] - 1 + 127, 0) - down, 1)
    scale = np.exp2(byte - 127.0)
    codes = (blocks / scale).astype(np.float32).astype(dtype).astype(np.float64)
    return np.moveaxis((codes * scale).reshape(v.shape), -1, axis)


WIDE = False


def mx_kscale(k):
    if not WIDE:
        return np.ones(k)
    levels = np.array([10, -10, 5, -5, 0])
    if k % 512:
        return np.exp2(np.random.permutation(np.resize(levels, k // 32))).repeat(32)
    a = np.empty((k // 512, 16))
    for p in range(k // 512):
        a[p, :8] = np.random.permutation(np.resize(levels, 8))
        for g in range(8):
            far = levels[np.abs(levels - a[p, g]) >= 10]
            a[p, g + 8] = far[np.random.randint(len(far))]
    return np.exp2(a.ravel()).repeat(32)


def f64(x):
    return np.asarray(x).astype(np.float64)


def striped(idx):
    return np.tile(idx.reshape(-1, 16).T, (8, 1)).astype(np.uint16)


def unstriped(offs):
    return offs[:16].T.reshape(-1).astype(np.int64)


def pack_weight(w):
    k, n = w.shape
    w = f64(np.asarray(w, np.float32).astype(ml_dtypes.bfloat16)).reshape(k // 32, 32, n)
    amax = np.abs(w).max(1)
    byte = np.clip(np.where(amax > 0, np.frexp(amax)[1] - 1 + 127 - 7, 1), 1, 254)
    scaled = (w * np.exp2(127.0 - byte)[:, None, :]).reshape(k, n).astype(np.float32)
    words = np.ascontiguousarray(scaled.reshape(k // 512, 128, 4, n).transpose(0, 1, 3, 2)).astype(ml_dtypes.float8_e4m3fn).view(np.uint8)
    return words, np.ascontiguousarray(byte.astype(np.uint8).reshape(k // 512, 16, n))


def unpack_weight(words, scales):
    g, p, n, _ = words.shape
    vals = np.ascontiguousarray(words).view(ml_dtypes.float8_e4m3fn).astype(np.float64) * np.repeat(np.exp2(scales.astype(np.float64) - 127.0), 8, axis=1)[..., None]
    return vals.transpose(0, 1, 3, 2).reshape(g * 512, n)


E2M1 = np.array([0.0, 0.5, 1.0, 1.5, 2.0, 3.0, 4.0, 6.0, -0.0, -0.5, -1.0, -1.5, -2.0, -3.0, -4.0, -6.0])


def pack_fp4(w):
    k, n = w.shape
    w = f64(np.asarray(w, np.float32).astype(ml_dtypes.bfloat16)).reshape(k // 32, 32, n)
    amax = np.abs(w).max(1)
    mant, ex = np.frexp(amax / 6.0)
    byte = np.clip(np.where(amax > 0, np.where(mant > 0.5, ex, ex - 1) + 127, 1), 1, 254)
    scaled = (w * np.exp2(127.0 - byte)[:, None, :]).reshape(k, n).astype(np.float32)
    c = np.ascontiguousarray(scaled.reshape(k // 512, 128, 4, n).transpose(0, 1, 3, 2)).astype(ml_dtypes.float4_e2m1fn).view(np.uint8) & 0xF
    words = (c[..., 0::2] | (c[..., 1::2] << 4)).reshape(k // 512, 128, 2 * n)
    return np.ascontiguousarray(words), np.ascontiguousarray(byte.astype(np.uint8).reshape(k // 512, 16, n))


def unpack_fp4(words, scales):
    g, _, n = scales.shape
    words = np.ascontiguousarray(words).reshape(g, 128, n, 2)
    nib = np.empty((g, 128, n, 4), np.uint8)
    nib[..., 0::2] = words & 0xF
    nib[..., 1::2] = words >> 4
    vals = E2M1[nib] * np.repeat(np.exp2(scales.astype(np.float64) - 127.0), 8, axis=1)[..., None]
    return vals.transpose(0, 1, 3, 2).reshape(g * 512, n)


def planes(y):
    n, m = y.shape
    v = y.astype(np.float32).astype(ml_dtypes.bfloat16).astype(np.float64).reshape(n // 32, 32, m)
    top = np.abs(v).max(1)
    byte = np.clip(np.where(top > 0, np.frexp(top)[1] - 1 + 127 - 7, 1), 1, 254)
    codes = (v * np.exp2(127.0 - byte)[:, None, :]).reshape(n, m).astype(np.float32).astype(ml_dtypes.float8_e4m3fn).view(np.uint8)
    words = codes.reshape(n // 512, 128, 4, m).transpose(0, 1, 3, 2)
    return np.ascontiguousarray(words), np.ascontiguousarray(byte.astype(np.uint8).reshape(n // 512, 16, m))


K, T, S, N, H, W = 512, 2048, 512, 512, 512, 384


def setup_inputs():
    n = np.random.standard_normal
    s = mx_kscale(K)[:, None]
    u = mx_kscale(H)
    packed_xT = pack_weight(n((K, T)) * s)
    packed_w1 = pack_fp4(n((K, H)) / np.sqrt(K) / s)
    packed_w2 = pack_fp4(n((H, N)) / np.sqrt(2 * H) / u[:, None])
    packed_w3 = pack_fp4(n((H, N)) / np.sqrt(2 * H) / u[:, None])
    return {
        "x_words": packed_xT[0],
        "x_scales": packed_xT[1],
        "w1_words": packed_w1[0],
        "w1_scales": packed_w1[1],
        "tau": np.random.uniform(0.3, 0.9, (H, 1)).astype(np.float32),
        "tau2": np.random.uniform(0.3, 0.9, (H, 1)).astype(np.float32),
        "gn": (np.random.uniform(0.5, 1.5, (H, 1)) * u[:, None]).astype(np.float32),
        "gm": (np.random.uniform(0.5, 1.5, (H, 1)) * u[:, None]).astype(np.float32),
        "w2_words": packed_w2[0],
        "w2_scales": packed_w2[1],
        "w3_words": packed_w3[0],
        "w3_scales": packed_w3[1],
        "tau3": np.random.uniform(0.5, 1.2, (N, 1)).astype(np.float32),
        "offs": striped(np.random.permutation(T)[:S]),
        "n1": striped(np.random.permutation(S)[:W]),
        "n2": striped(np.random.permutation(S)[:W]),
        "n3": striped(np.random.permutation(S)),
        "n4": striped(np.random.permutation(S)),
        "n5": striped(np.random.permutation(S)),
        "n6": striped(np.random.permutation(S)),
    }


def reference(x_words, x_scales, w1_words, w1_scales, tau, tau2, gn, gm, w2_words, w2_scales, w3_words, w3_scales, tau3, offs, n1, n2, n3, n4, n5, n6):
    xq = unpack_weight(x_words, x_scales)[:, unstriped(offs)]
    y = unpack_fp4(w1_words, w1_scales).T @ xq
    pa = y[:, unstriped(n2)]
    old = y[:, unstriped(n1)]
    ra = np.maximum(pa, 0.5 * old)
    ds = y.copy()
    ds[:, unstriped(n1)] = ra
    z = f64(gn) * ds
    top = y.max(axis=1, keepdims=True)
    ea = np.exp(f64(tau) * (y[:, unstriped(n3)] - top))
    low = y.min(axis=1, keepdims=True)
    ea2 = np.exp(f64(tau2) * (low - y[:, unstriped(n4)]))
    z2 = f64(gm) * (1.5 * (y * (ea + ea2)))
    h = unpack_fp4(w2_words, w2_scales).T @ mxq(z, 0, "e4m3") + unpack_fp4(w3_words, w3_scales).T @ mxq(z2, 0, "e4m3")
    sz = np.abs(h)
    ea3 = np.exp(-1.0 * (f64(tau3) * sz[:, unstriped(n5)]))
    out_0 = (h - h[:, unstriped(n6)]) * ea3
    return (out_0,) + planes(out_0)

@@ -1,0 +1,272 @@
+from contextlib import ExitStack
+
+import concourse.mybir as mybir
+
+K, T, S, H, N, W = 512, 2048, 512, 512, 512, 384
+FLOPS = 2 * K * H * S + 2 * 2 * H * N * S
+
+F32 = mybir.dt.float32
+BF16 = mybir.dt.bfloat16
+I32 = mybir.dt.int32
+U32 = mybir.dt.uint32
+U16 = mybir.dt.uint16
+U8 = mybir.dt.uint8
+FP8X4 = mybir.dt.float8_e4m3fn_x4
+FP4X4 = mybir.dt.float4_e2m1fn_x4
+ALU = mybir.AluOpType
+ACT = mybir.ActivationFunctionType
+
+P = 128
+PACK = 4
+QUADS = 4
+HALF = S // 2
+LIST_COL = 16
+RUN = 4
+
+
+def tile_picked_joinkmaxedfela_none_po_kernel(
+    tc, x_words, x_scales, w1_words, w1_scales, tau, tau2, gn, gm,
+    w2_words, w2_scales, w3_words, w3_scales, tau3,
+    offs, n1, n2, n3, n4, n5, n6, out_0, out_1, out_2,
+):
+    nc = tc.nc
+    with ExitStack() as ctx:
+        keep = ctx.enter_context(tc.tile_pool(name="keep", bufs=1))
+        psum = ctx.enter_context(tc.psum_pool(name="psum", bufs=1))
+
+        def sbuf(name, shape, dtype, tag=None):
+            return keep.tile(shape, dtype, name=name, tag=tag or name, align_bytes=64)
+
+        def load_list(name, src):
+            tile = keep.tile(list(src.shape), U16, name=name)
+            nc.sync.dma_start(tile[:], src)
+            return tile
+
+        def load_scale_rows(queue, plane, src, q):
+            queue.dma_start(plane[32 * q : 32 * q + 4, :].bitcast(I32), src[0, 4 * q : 4 * q + 4, :].bitcast(I32))
+
+        def load_column(name, src):
+            tile = sbuf(name, [P, PACK], F32)
+            nc.gpsimd.dma_start(tile[:], src.rearrange("(p t) o -> p (t o)", t=PACK))
+            return tile
+
+        def list_half(tile, h):
+            cols = HALF // LIST_COL
+            return tile[:, h * cols : (h + 1) * cols]
+
+        def interleave(engine_copy, grouped, planes):
+            engine_copy(
+                grouped[:].rearrange("p (c i t) -> p c t i", i=RUN, t=PACK),
+                planes.rearrange("p t (c i) -> p c t i", i=RUN),
+            )
+
+        w1s_raw = sbuf("w1s_raw", [P, H], U8)
+        xs_raw = sbuf("xs_raw", [P, T], U8, tag="x_bytes_then_words")
+        w23s_raw = sbuf("w23s_raw", [P, 2 * N], U8)
+        nc.gpsimd.memset(xs_raw[:].bitcast(I32), 0)
+        nc.vector.memset(w1s_raw[:].bitcast(I32), 0)
+        nc.vector.memset(w23s_raw[:].bitcast(I32), 0)
+
+        offs_sb = load_list("offs_sb", offs)
+        w1w_raw = sbuf("w1w_raw", [P, 2 * H], U8)
+        nc.sync.dma_start(w1w_raw[:].bitcast(I32), w1_words[0].bitcast(I32))
+        xw_raw = sbuf("xw_raw", [P, T], U32)
+        nc.sync.dma_start(xw_raw[:].bitcast(I32), x_words[0].rearrange("p n r -> p (n r)").bitcast(I32))
+        for q in range(QUADS):
+            load_scale_rows(nc.scalar, xs_raw, x_scales, q)
+        for q in range(QUADS - 1):
+            load_scale_rows(nc.scalar, w1s_raw, w1_scales, q)
+        load_scale_rows(nc.gpsimd, w1s_raw, w1_scales, QUADS - 1)
+        tau_sb = load_column("tau_sb", tau)
+        tau2_sb = load_column("tau2_sb", tau2)
+        gm_sb = load_column("gm_sb", gm)
+        gn_sb = load_column("gn_sb", gn)
+        tau3_sb = load_column("tau3_sb", tau3)
+        n1_sb = load_list("n1_sb", n1)
+        n2_sb = load_list("n2_sb", n2)
+        n3_sb = load_list("n3_sb", n3)
+        n4_sb = load_list("n4_sb", n4)
+        w23w_raw = sbuf("w23w_raw", [P, 2 * 2 * N], U8)
+        for a, (words, scales) in enumerate(((w2_words, w2_scales), (w3_words, w3_scales))):
+            nc.sync.dma_start(w23w_raw[:, a * 2 * N : (a + 1) * 2 * N].bitcast(I32), words[0].bitcast(I32))
+        for a, (words, scales) in enumerate(((w2_words, w2_scales), (w3_words, w3_scales))):
+            for q in range(QUADS):
+                load_scale_rows(nc.sync, w23s_raw[:, a * N : (a + 1) * N], scales, q)
+        n5_sb = load_list("n5_sb", n5)
+        n6_sb = load_list("n6_sb", n6)
+
+        w1w = sbuf("w1w", [P, 2 * H], U8)
+        w1s = sbuf("w1s", [P, H], U8)
+        nc.vector.tensor_copy(
+            w1w[:].rearrange("p (t m b) -> p t m b", t=PACK, b=2),
+            w1w_raw[:].rearrange("p (m t b) -> p t m b", t=PACK, b=2),
+        )
+        xs = sbuf("xs", [P, S], U8)
+        nc.vector.tensor_copy(xs[:], xs_raw[:].indirect(offs_sb[:]))
+        nc.vector.tensor_copy(
+            w1s[:].rearrange("p (t m) -> p t m", t=PACK),
+            w1s_raw[:].rearrange("p (m t) -> p t m", t=PACK),
+        )
+        xw = sbuf("xw", [P, S], U32, tag="x_bytes_then_words")
+        nc.vector.tensor_copy(xw[:], xw_raw[:].indirect(offs_sb[:]))
+
+        rates = sbuf("rates", [P, PACK, 2], F32)
+        neg_tau2 = sbuf("neg_tau2", [P, PACK], F32)
+        neg_tau3 = sbuf("neg_tau3", [P, PACK], F32)
+        gm15 = sbuf("gm15", [P, PACK], F32)
+        nc.scalar.activation(rates[:, :, 0], tau_sb[:], ACT.Copy, scale=-1.0)
+        nc.scalar.activation(rates[:, :, 1], tau2_sb[:], ACT.Copy)
+        nc.scalar.activation(neg_tau2[:], tau2_sb[:], ACT.Copy, scale=-1.0)
+        nc.scalar.activation(gm15[:], gm_sb[:], ACT.Copy, scale=1.5)
+        nc.scalar.activation(neg_tau3[:], tau3_sb[:], ACT.Copy, scale=-1.0)
+
+        w23w = sbuf("w23w", [P, 2 * 2 * N], U8)
+        w23s = sbuf("w23s", [P, 2 * N], U8)
+        nc.scalar.copy(
+            w23w[:].bitcast(U16).rearrange("p (a t m) -> p a t m", a=2, t=PACK),
+            w23w_raw[:].bitcast(U16).rearrange("p (a m t) -> p a t m", a=2, t=PACK),
+        )
+
+        y_ps = []
+        for t in range(PACK):
+            bank = psum.tile([P, S], F32, name="y_ps%d" % t, tag="bank%d" % t)
+            nc.tensor.matmul_mx(
+                bank[:],
+                lhsT=w1w[:, 2 * P * t : 2 * P * (t + 1)].bitcast(FP4X4),
+                lhsT_scale=w1s[:, P * t : P * (t + 1)],
+                rhs=xw[:].bitcast(FP8X4),
+                rhs_scale=xs[:],
+                start=True,
+                stop=True,
+            )
+            y_ps.append(bank)
+        nc.vector.tensor_copy(
+            w23s[:].rearrange("p (a t m) -> p a t m", a=2, t=PACK),
+            w23s_raw[:].rearrange("p (a m t) -> p a t m", a=2, t=PACK),
+        )
+
+        ends = sbuf("ends", [P, PACK, 2], F32)
+        biases = sbuf("biases", [P, PACK, 2], F32)
+        y = [sbuf("y%d" % t, [P, S], F32) for t in range(PACK)]
+        ds = [sbuf("ds%d" % t, [P, S], F32) for t in range(PACK)]
+        z_planes = sbuf("z_planes", [P, PACK, S], BF16)
+
+        def exp_pair(pair, t, h):
+            col = slice(t, t + 1)
+            nc.scalar.activation(pair[:, 0, t, :], y[t][:].indirect(list_half(n3_sb, h)), ACT.Exp,
+                                 bias=biases[:, t, 0:1], scale=tau_sb[:, col])
+            nc.scalar.activation(pair[:, 1, t, :], y[t][:].indirect(list_half(n4_sb, h)), ACT.Exp,
+                                 bias=biases[:, t, 1:2], scale=neg_tau2[:, col])
+
+        pairs = [sbuf("pair0", [P, 2, PACK, HALF], F32)]
+        z2_planes = [sbuf("z2_planes%d" % h, [P, PACK, HALF], BF16) for h in range(2)]
+
+        def z2_plane(t, h):
+            nc.vector.tensor_tensor(pairs[h][:, 0, t, :], pairs[h][:, 0, t, :], pairs[h][:, 1, t, :], ALU.add)
+            nc.vector.scalar_tensor_tensor(z2_planes[h][:, t, :], pairs[h][:, 0, t, :], gm15[:, t : t + 1],
+                                           y[t][:, h * HALF : (h + 1) * HALF], ALU.mult, ALU.mult)
+
+        def z_plane(t):
+            nc.vector.tensor_scalar(z_planes[:, t, :], ds[t][:], gn_sb[:, t : t + 1], None, ALU.mult)
+
+        for t in range(PACK):
+            nc.vector.tensor_scalar(y[t][:], y_ps[t][:], 1.0, None, ALU.mult, ALU.max, accum_out=ends[:, t, 0:1])
+            nc.vector.tensor_scalar(ds[t][:], y_ps[t][:], 1.0, None, ALU.mult, ALU.min, accum_out=ends[:, t, 1:2])
+            pa = sbuf("pa%d" % t, [P, W], F32)
+            old = sbuf("old%d" % t, [P, W], F32)
+            ra = sbuf("ra%d" % t, [P, W], F32, tag="last_ra_then_pair" if t == PACK - 1 else None)
+            nc.vector.tensor_tensor(biases[:, t, :], ends[:, t, :], rates[:, t, :], ALU.mult)
+            if t % 2 == 0:
+                nc.scalar.activation(old[:], y[t][:].indirect(n1_sb[:]), ACT.Copy)
+            else:
+                nc.vector.tensor_copy(old[:], y[t][:].indirect(n1_sb[:]))
+            nc.vector.tensor_copy(pa[:], y[t][:].indirect(n2_sb[:]))
+            if t == 2:
+                z_plane(0)
+                z2_plane(0, 0)
+            nc.vector.scalar_tensor_tensor(ra[:], old[:], 0.5, pa[:], ALU.mult, ALU.max)
+            exp_pair(pairs[0], t, 0)
+            nc.scalar.activation(ds[t][:].indirect(n1_sb[:]), ra[:], ACT.Copy)
+        pairs.append(sbuf("pair1", [P, 2, PACK, HALF], F32, tag="last_ra_then_pair"))
+        for t in range(PACK):
+            exp_pair(pairs[1], t, 1)
+
+        def quantise(name, planes, words, scales, copy):
+            grouped = sbuf(name, [P, HALF * PACK], BF16)
+            interleave(copy, grouped, planes)
+            nc.vector.quantize_mx(words.bitcast(FP8X4), scales, grouped[:])
+
+        def z2_half(h):
+            words = sbuf("z2_words%d" % h, [P, HALF], U32)
+            scales = sbuf("z2_scales%d" % h, [P, HALF], U8)
+            quantise("z2_grouped%d" % h, z2_planes[h][:], words[:], scales[:], nc.vector.tensor_copy)
+            return words, scales
+
+        def z_half(h):
+            cols = slice(h * HALF, (h + 1) * HALF)
+            words = sbuf("z_words%d" % h, [P, HALF], U32)
+            scales = sbuf("z_scales%d" % h, [P, HALF], U8)
+            quantise("z_grouped%d" % h, z_planes[:, :, cols], words[:], scales[:], nc.vector.tensor_copy)
+            return words, scales
+
+        hsb = [sbuf("h%d" % t, [P, S], F32) for t in range(PACK)]
+        h_plain = [sbuf("h_plain%d" % t, [P, S], F32) for t in range(PACK)]
+        sz = [sbuf("sz%d" % t, [P, S], F32) for t in range(PACK)]
+
+        def second_product(h, operands):
+            cols = slice(h * HALF, (h + 1) * HALF)
+            banks = [psum.tile([P, HALF], F32, name="h_ps%d_%d" % (h, t), tag="bank%d" % (PACK * (1 - h) + t))
+                     for t in range(PACK)]
+            for i, (a, (words, scales)) in enumerate(operands):
+                for t in range(PACK):
+                    nc.tensor.matmul_mx(
+                        banks[t][:],
+                        lhsT=w23w[:, 2 * (N * a + P * t) : 2 * (N * a + P * (t + 1))].bitcast(FP4X4),
+                        lhsT_scale=w23s[:, N * a + P * t : N * a + P * (t + 1)],
+                        rhs=words[:].bitcast(FP8X4),
+                        rhs_scale=scales[:],
+                        start=(i == 0),
+                        stop=(i == 1),
+                    )
+            for t in range(PACK):
+                nc.scalar.activation(hsb[t][:, cols], banks[t][:], ACT.Copy, scale=-1.0)
+                if h == 1:
+                    nc.scalar.activation(sz[t][:, cols], banks[t][:], ACT.Abs)
+                nc.sync.dma_start(h_plain[t][:, cols], hsb[t][:, cols])
+            return banks
+
+        for t in range(1, PACK):
+            z2_plane(t, 0)
+        z2_first = z2_half(0)
+        for t in range(1, PACK):
+            z_plane(t)
+        first_banks = second_product(0, ((1, z2_first), (0, z_half(0))))
+        z_second = z_half(1)
+        for t in range(PACK):
+            z2_plane(t, 1)
+        second_product(1, ((0, z_second), (1, z2_half(1))))
+        for t in range(PACK):
+            nc.vector.tensor_tensor(sz[t][:, 0:HALF], first_banks[t][:], hsb[t][:, 0:HALF], ALU.max)
+
+        out_rows = out_0.rearrange("(p t) c -> p t c", t=PACK)
+        out_words = out_1[0].rearrange("p c r -> p (c r)").bitcast(I32)
+        o_words = sbuf("o_words", [P, S], U32)
+        o_scales = sbuf("o_scales", [P, S], U8)
+        for h in range(2):
+            cols = slice(h * HALF, (h + 1) * HALF)
+            result = sbuf("result%d" % h, [P, PACK, HALF], F32)
+            ea3 = sbuf("ea3_%d" % h, [P, PACK, HALF], F32)
+            diff = sbuf("diff%d" % h, [P, PACK, HALF], F32)
+            for t in range(PACK):
+                nc.scalar.activation(ea3[:, t, :], sz[t][:].indirect(list_half(n5_sb, h)), ACT.Exp, scale=neg_tau3[:, t : t + 1])
+                nc.vector.tensor_tensor(diff[:, t, :], hsb[t][:].indirect(list_half(n6_sb, h)), h_plain[t][:, cols], ALU.subtract)
+                if t % 2 == 1:
+                    two = slice(t - 1, t + 1)
+                    nc.vector.tensor_tensor(result[:, two, :], diff[:, two, :], ea3[:, two, :], ALU.mult)
+            nc.sync.dma_start(out_rows[:, :, cols], result[:])
+            quantise("o_grouped%d" % h, result[:], o_words[:, cols], o_scales[:, cols],
+                     nc.scalar.copy if h == 0 else nc.vector.tensor_copy)
+            nc.sync.dma_start(out_words[:, cols], o_words[:, cols].bitcast(I32))
+        for q in range(QUADS):
+            queue = nc.sync if q % 2 == 0 else nc.scalar
+            queue.dma_start(out_2[0, 4 * q : 4 * q + 4, :].bitcast(I32), o_scales[32 * q : 32 * q + 4, :].bitcast(I32))

@@ -42,8 +42,9 @@ def tile_picked_joinkmaxedfela_none_po_kernel(
             nc.sync.dma_start(tile[:], src)
             return tile
 
-        def load_scale_rows(queue, plane, src, q):
-            queue.dma_start(plane[32 * q : 32 * q + 4, :].bitcast(I32), src[0, 4 * q : 4 * q + 4, :].bitcast(I32))
+        def load_scale_rows(plane, src):
+            for q in range(QUADS):
+                nc.sync.dma_start(plane[32 * q : 32 * q + 4, :].bitcast(I32), src[0, 4 * q : 4 * q + 4, :].bitcast(I32))
 
         def load_column(name, src):
             tile = sbuf(name, [P, PACK], F32)
@@ -64,51 +65,47 @@ def tile_picked_joinkmaxedfela_none_po_kernel(
         xs_raw = sbuf("xs_raw", [P, T], U8, tag="x_bytes_then_words")
         w23s_raw = sbuf("w23s_raw", [P, 2 * N], U8)
         nc.gpsimd.memset(xs_raw[:].bitcast(I32), 0)
-        nc.vector.memset(w1s_raw[:].bitcast(I32), 0)
+        nc.gpsimd.memset(w1s_raw[:].bitcast(I32), 0)
         nc.vector.memset(w23s_raw[:].bitcast(I32), 0)
 
         offs_sb = load_list("offs_sb", offs)
-        w1w_raw = sbuf("w1w_raw", [P, 2 * H], U8)
-        nc.sync.dma_start(w1w_raw[:].bitcast(I32), w1_words[0].bitcast(I32))
+        n1_sb = load_list("n1_sb", n1)
+        load_scale_rows(xs_raw, x_scales)
         xw_raw = sbuf("xw_raw", [P, T], U32)
         nc.sync.dma_start(xw_raw[:].bitcast(I32), x_words[0].rearrange("p n r -> p (n r)").bitcast(I32))
-        for q in range(QUADS):
-            load_scale_rows(nc.scalar, xs_raw, x_scales, q)
-        for q in range(QUADS - 1):
-            load_scale_rows(nc.scalar, w1s_raw, w1_scales, q)
-        load_scale_rows(nc.gpsimd, w1s_raw, w1_scales, QUADS - 1)
+        w1w_raw = sbuf("w1w_raw", [P, 2 * H], U8)
+        nc.sync.dma_start(w1w_raw[:].bitcast(I32), w1_words[0].bitcast(I32))
+        load_scale_rows(w1s_raw, w1_scales)
+        w23w_raw = sbuf("w23w_raw", [P, 2 * 2 * N], U8)
+        for a, words in enumerate((w2_words, w3_words)):
+            nc.sync.dma_start(w23w_raw[:, a * 2 * N : (a + 1) * 2 * N].bitcast(I32), words[0].bitcast(I32))
+        n2_sb = load_list("n2_sb", n2)
+        n3_sb = load_list("n3_sb", n3)
+        n4_sb = load_list("n4_sb", n4)
+        for a, scales in enumerate((w2_scales, w3_scales)):
+            load_scale_rows(w23s_raw[:, a * N : (a + 1) * N], scales)
+        n5_sb = load_list("n5_sb", n5)
+        n6_sb = load_list("n6_sb", n6)
         tau_sb = load_column("tau_sb", tau)
         tau2_sb = load_column("tau2_sb", tau2)
         gm_sb = load_column("gm_sb", gm)
         gn_sb = load_column("gn_sb", gn)
         tau3_sb = load_column("tau3_sb", tau3)
-        n1_sb = load_list("n1_sb", n1)
-        n2_sb = load_list("n2_sb", n2)
-        n3_sb = load_list("n3_sb", n3)
-        n4_sb = load_list("n4_sb", n4)
-        w23w_raw = sbuf("w23w_raw", [P, 2 * 2 * N], U8)
-        for a, (words, scales) in enumerate(((w2_words, w2_scales), (w3_words, w3_scales))):
-            nc.sync.dma_start(w23w_raw[:, a * 2 * N : (a + 1) * 2 * N].bitcast(I32), words[0].bitcast(I32))
-        for a, (words, scales) in enumerate(((w2_words, w2_scales), (w3_words, w3_scales))):
-            for q in range(QUADS):
-                load_scale_rows(nc.sync, w23s_raw[:, a * N : (a + 1) * N], scales, q)
-        n5_sb = load_list("n5_sb", n5)
-        n6_sb = load_list("n6_sb", n6)
 
         w1w = sbuf("w1w", [P, 2 * H], U8)
         w1s = sbuf("w1s", [P, H], U8)
-        nc.vector.tensor_copy(
-            w1w[:].rearrange("p (t m b) -> p t m b", t=PACK, b=2),
-            w1w_raw[:].rearrange("p (m t b) -> p t m b", t=PACK, b=2),
+        nc.scalar.copy(
+            w1w[:].bitcast(U16).rearrange("p (t m) -> p t m", t=PACK),
+            w1w_raw[:].bitcast(U16).rearrange("p (m t) -> p t m", t=PACK),
         )
         xs = sbuf("xs", [P, S], U8)
         nc.vector.tensor_copy(xs[:], xs_raw[:].indirect(offs_sb[:]))
+        xw = sbuf("xw", [P, S], U32, tag="x_bytes_then_words")
+        nc.vector.tensor_copy(xw[:], xw_raw[:].indirect(offs_sb[:]))
         nc.vector.tensor_copy(
             w1s[:].rearrange("p (t m) -> p t m", t=PACK),
             w1s_raw[:].rearrange("p (m t) -> p t m", t=PACK),
         )
-        xw = sbuf("xw", [P, S], U32, tag="x_bytes_then_words")
-        nc.vector.tensor_copy(xw[:], xw_raw[:].indirect(offs_sb[:]))
 
         rates = sbuf("rates", [P, PACK, 2], F32)
         neg_tau2 = sbuf("neg_tau2", [P, PACK], F32)
@@ -140,10 +137,11 @@ def tile_picked_joinkmaxedfela_none_po_kernel(
                 stop=True,
             )
             y_ps.append(bank)
-        nc.vector.tensor_copy(
-            w23s[:].rearrange("p (a t m) -> p a t m", a=2, t=PACK),
-            w23s_raw[:].rearrange("p (a m t) -> p a t m", a=2, t=PACK),
-        )
+        for a in range(2):
+            nc.vector.tensor_copy(
+                w23s[:, a * N : (a + 1) * N].rearrange("p (t m) -> p t m", t=PACK),
+                w23s_raw[:, a * N : (a + 1) * N].rearrange("p (m t) -> p t m", t=PACK),
+            )
 
         ends = sbuf("ends", [P, PACK, 2], F32)
         biases = sbuf("biases", [P, PACK, 2], F32)
@@ -176,17 +174,20 @@ def tile_picked_joinkmaxedfela_none_po_kernel(
             old = sbuf("old%d" % t, [P, W], F32)
             ra = sbuf("ra%d" % t, [P, W], F32, tag="last_ra_then_pair" if t == PACK - 1 else None)
             nc.vector.tensor_tensor(biases[:, t, :], ends[:, t, :], rates[:, t, :], ALU.mult)
-            if t % 2 == 0:
+            if t in (0,1):
                 nc.scalar.activation(old[:], y[t][:].indirect(n1_sb[:]), ACT.Copy)
             else:
                 nc.vector.tensor_copy(old[:], y[t][:].indirect(n1_sb[:]))
-            nc.vector.tensor_copy(pa[:], y[t][:].indirect(n2_sb[:]))
-            if t == 2:
-                z_plane(0)
-                z2_plane(0, 0)
+            if t in ():
+                nc.scalar.activation(pa[:], y[t][:].indirect(n2_sb[:]), ACT.Copy)
+            else:
+                nc.vector.tensor_copy(pa[:], y[t][:].indirect(n2_sb[:]))
             nc.vector.scalar_tensor_tensor(ra[:], old[:], 0.5, pa[:], ALU.mult, ALU.max)
             exp_pair(pairs[0], t, 0)
-            nc.scalar.activation(ds[t][:].indirect(n1_sb[:]), ra[:], ACT.Copy)
+            if t in (3,):
+                nc.vector.tensor_copy(ds[t][:].indirect(n1_sb[:]), ra[:])
+            else:
+                nc.scalar.activation(ds[t][:].indirect(n1_sb[:]), ra[:], ACT.Copy)
         pairs.append(sbuf("pair1", [P, 2, PACK, HALF], F32, tag="last_ra_then_pair"))
         for t in range(PACK):
             exp_pair(pairs[1], t, 1)
@@ -228,25 +229,29 @@ def tile_picked_joinkmaxedfela_none_po_kernel(
                         start=(i == 0),
                         stop=(i == 1),
                     )
-            for t in range(PACK):
-                nc.scalar.activation(hsb[t][:, cols], banks[t][:], ACT.Copy, scale=-1.0)
-                if h == 1:
-                    nc.scalar.activation(sz[t][:, cols], banks[t][:], ACT.Abs)
-                nc.sync.dma_start(h_plain[t][:, cols], hsb[t][:, cols])
             return banks
 
-        for t in range(1, PACK):
+        def negated_h(t, h, bank):
+            cols = slice(h * HALF, (h + 1) * HALF)
+            nc.scalar.activation(hsb[t][:, cols], bank[:], ACT.Copy, scale=-1.0)
+            nc.sync.dma_start(h_plain[t][:, cols], hsb[t][:, cols])
+
+        for t in range(PACK):
             z2_plane(t, 0)
         z2_first = z2_half(0)
-        for t in range(1, PACK):
+        for t in range(PACK):
             z_plane(t)
         first_banks = second_product(0, ((1, z2_first), (0, z_half(0))))
-        z_second = z_half(1)
+        for t in range(PACK):
+            negated_h(t, 0, first_banks[t])
+        for t in range(PACK):
+            nc.scalar.activation(sz[t][:, 0:HALF], first_banks[t][:], ACT.Abs)
         for t in range(PACK):
             z2_plane(t, 1)
-        second_product(1, ((0, z_second), (1, z2_half(1))))
+        second_banks = second_product(1, ((0, z_half(1)), (1, z2_half(1))))
+
         for t in range(PACK):
-            nc.vector.tensor_tensor(sz[t][:, 0:HALF], first_banks[t][:], hsb[t][:, 0:HALF], ALU.max)
+            negated_h(t, 1, second_banks[t])
 
         out_rows = out_0.rearrange("(p t) c -> p t c", t=PACK)
         out_words = out_1[0].rearrange("p c r -> p (c r)").bitcast(I32)
@@ -258,12 +263,14 @@ def tile_picked_joinkmaxedfela_none_po_kernel(
             ea3 = sbuf("ea3_%d" % h, [P, PACK, HALF], F32)
             diff = sbuf("diff%d" % h, [P, PACK, HALF], F32)
             for t in range(PACK):
+                if h == 0:
+                    nc.scalar.activation(sz[t][:, HALF:S], second_banks[t][:], ACT.Abs)
                 nc.scalar.activation(ea3[:, t, :], sz[t][:].indirect(list_half(n5_sb, h)), ACT.Exp, scale=neg_tau3[:, t : t + 1])
                 nc.vector.tensor_tensor(diff[:, t, :], hsb[t][:].indirect(list_half(n6_sb, h)), h_plain[t][:, cols], ALU.subtract)
                 if t % 2 == 1:
                     two = slice(t - 1, t + 1)
                     nc.vector.tensor_tensor(result[:, two, :], diff[:, two, :], ea3[:, two, :], ALU.mult)
-            nc.sync.dma_start(out_rows[:, :, cols], result[:])
+                    nc.sync.dma_start(out_rows[:, two, cols], result[:, two, :])
             quantise("o_grouped%d" % h, result[:], o_words[:, cols], o_scales[:, cols],
                      nc.scalar.copy if h == 0 else nc.vector.tensor_copy)
             nc.sync.dma_start(out_words[:, cols], o_words[:, cols].bitcast(I32))

from contextlib import ExitStack

import concourse.mybir as mybir

K, T, S, H, N, W = 512, 2048, 512, 512, 512, 384
FLOPS = 2 * K * H * S + 2 * 2 * H * N * S

F32 = mybir.dt.float32
BF16 = mybir.dt.bfloat16
I32 = mybir.dt.int32
U32 = mybir.dt.uint32
U16 = mybir.dt.uint16
U8 = mybir.dt.uint8
FP8X4 = mybir.dt.float8_e4m3fn_x4
FP4X4 = mybir.dt.float4_e2m1fn_x4
ALU = mybir.AluOpType
ACT = mybir.ActivationFunctionType

P = 128
PACK = 4
QUADS = 4
HALF = S // 2
LIST_COL = 16
RUN = 4


def tile_picked_joinkmaxedfela_none_po_kernel(
    tc, x_words, x_scales, w1_words, w1_scales, tau, tau2, gn, gm,
    w2_words, w2_scales, w3_words, w3_scales, tau3,
    offs, n1, n2, n3, n4, n5, n6, out_0, out_1, out_2,
):
    nc = tc.nc
    with ExitStack() as ctx:
        keep = ctx.enter_context(tc.tile_pool(name="keep", bufs=1))
        psum = ctx.enter_context(tc.psum_pool(name="psum", bufs=1))

        def sbuf(name, shape, dtype, tag=None):
            return keep.tile(shape, dtype, name=name, tag=tag or name, align_bytes=64)

        def load_list(name, src):
            tile = keep.tile(list(src.shape), U16, name=name)
            nc.sync.dma_start(tile[:], src)
            return tile

        def load_scale_rows(plane, src):
            for q in range(QUADS):
                nc.sync.dma_start(plane[32 * q : 32 * q + 4, :].bitcast(I32), src[0, 4 * q : 4 * q + 4, :].bitcast(I32))

        def load_column(name, src):
            tile = sbuf(name, [P, PACK], F32)
            nc.gpsimd.dma_start(tile[:], src.rearrange("(p t) o -> p (t o)", t=PACK))
            return tile

        def list_half(tile, h):
            cols = HALF // LIST_COL
            return tile[:, h * cols : (h + 1) * cols]

        def interleave(engine_copy, grouped, planes):
            engine_copy(
                grouped[:].rearrange("p (c i t) -> p c t i", i=RUN, t=PACK),
                planes.rearrange("p t (c i) -> p c t i", i=RUN),
            )

        w1s_raw = sbuf("w1s_raw", [P, H], U8)
        xs_raw = sbuf("xs_raw", [P, T], U8, tag="x_bytes_then_words")
        w23s_raw = sbuf("w23s_raw", [P, 2 * N], U8)
        nc.gpsimd.memset(xs_raw[:].bitcast(I32), 0)
        nc.gpsimd.memset(w1s_raw[:].bitcast(I32), 0)
        nc.vector.memset(w23s_raw[:].bitcast(I32), 0)

        offs_sb = load_list("offs_sb", offs)
        n1_sb = load_list("n1_sb", n1)
        load_scale_rows(xs_raw, x_scales)
        xw_raw = sbuf("xw_raw", [P, T], U32)
        nc.sync.dma_start(xw_raw[:].bitcast(I32), x_words[0].rearrange("p n r -> p (n r)").bitcast(I32))
        w1w_raw = sbuf("w1w_raw", [P, 2 * H], U8)
        nc.sync.dma_start(w1w_raw[:].bitcast(I32), w1_words[0].bitcast(I32))
        load_scale_rows(w1s_raw, w1_scales)
        w23w_raw = sbuf("w23w_raw", [P, 2 * 2 * N], U8)
        for a, words in enumerate((w2_words, w3_words)):
            nc.sync.dma_start(w23w_raw[:, a * 2 * N : (a + 1) * 2 * N].bitcast(I32), words[0].bitcast(I32))
        n2_sb = load_list("n2_sb", n2)
        n3_sb = load_list("n3_sb", n3)
        n4_sb = load_list("n4_sb", n4)
        for a, scales in enumerate((w2_scales, w3_scales)):
            load_scale_rows(w23s_raw[:, a * N : (a + 1) * N], scales)
        n5_sb = load_list("n5_sb", n5)
        n6_sb = load_list("n6_sb", n6)
        tau_sb = load_column("tau_sb", tau)
        tau2_sb = load_column("tau2_sb", tau2)
        gm_sb = load_column("gm_sb", gm)
        gn_sb = load_column("gn_sb", gn)
        tau3_sb = load_column("tau3_sb", tau3)

        w1w = sbuf("w1w", [P, 2 * H], U8)
        w1s = sbuf("w1s", [P, H], U8)
        nc.scalar.copy(
            w1w[:].bitcast(U16).rearrange("p (t m) -> p t m", t=PACK),
            w1w_raw[:].bitcast(U16).rearrange("p (m t) -> p t m", t=PACK),
        )
        xs = sbuf("xs", [P, S], U8)
        nc.vector.tensor_copy(xs[:], xs_raw[:].indirect(offs_sb[:]))
        xw = sbuf("xw", [P, S], U32, tag="x_bytes_then_words")
        nc.vector.tensor_copy(xw[:], xw_raw[:].indirect(offs_sb[:]))
        nc.vector.tensor_copy(
            w1s[:].rearrange("p (t m) -> p t m", t=PACK),
            w1s_raw[:].rearrange("p (m t) -> p t m", t=PACK),
        )

        rates = sbuf("rates", [P, PACK, 2], F32)
        neg_tau2 = sbuf("neg_tau2", [P, PACK], F32)
        neg_tau3 = sbuf("neg_tau3", [P, PACK], F32)
        gm15 = sbuf("gm15", [P, PACK], F32)
        nc.scalar.activation(rates[:, :, 0], tau_sb[:], ACT.Copy, scale=-1.0)
        nc.scalar.activation(rates[:, :, 1], tau2_sb[:], ACT.Copy)
        nc.scalar.activation(neg_tau2[:], tau2_sb[:], ACT.Copy, scale=-1.0)
        nc.scalar.activation(gm15[:], gm_sb[:], ACT.Copy, scale=1.5)
        nc.scalar.activation(neg_tau3[:], tau3_sb[:], ACT.Copy, scale=-1.0)

        w23w = sbuf("w23w", [P, 2 * 2 * N], U8)
        w23s = sbuf("w23s", [P, 2 * N], U8)
        nc.scalar.copy(
            w23w[:].bitcast(U16).rearrange("p (a t m) -> p a t m", a=2, t=PACK),
            w23w_raw[:].bitcast(U16).rearrange("p (a m t) -> p a t m", a=2, t=PACK),
        )

        y_ps = []
        for t in range(PACK):
            bank = psum.tile([P, S], F32, name="y_ps%d" % t, tag="bank%d" % t)
            nc.tensor.matmul_mx(
                bank[:],
                lhsT=w1w[:, 2 * P * t : 2 * P * (t + 1)].bitcast(FP4X4),
                lhsT_scale=w1s[:, P * t : P * (t + 1)],
                rhs=xw[:].bitcast(FP8X4),
                rhs_scale=xs[:],
                start=True,
                stop=True,
            )
            y_ps.append(bank)
        for a in range(2):
            nc.vector.tensor_copy(
                w23s[:, a * N : (a + 1) * N].rearrange("p (t m) -> p t m", t=PACK),
                w23s_raw[:, a * N : (a + 1) * N].rearrange("p (m t) -> p t m", t=PACK),
            )

        ends = sbuf("ends", [P, PACK, 2], F32)
        biases = sbuf("biases", [P, PACK, 2], F32)
        y = [sbuf("y%d" % t, [P, S], F32) for t in range(PACK)]
        ds = [sbuf("ds%d" % t, [P, S], F32) for t in range(PACK)]
        z_planes = sbuf("z_planes", [P, PACK, S], BF16)

        def exp_pair(pair, t, h):
            col = slice(t, t + 1)
            nc.scalar.activation(pair[:, 0, t, :], y[t][:].indirect(list_half(n3_sb, h)), ACT.Exp,
                                 bias=biases[:, t, 0:1], scale=tau_sb[:, col])
            nc.scalar.activation(pair[:, 1, t, :], y[t][:].indirect(list_half(n4_sb, h)), ACT.Exp,
                                 bias=biases[:, t, 1:2], scale=neg_tau2[:, col])

        pairs = [sbuf("pair0", [P, 2, PACK, HALF], F32)]
        z2_planes = [sbuf("z2_planes%d" % h, [P, PACK, HALF], BF16) for h in range(2)]

        def z2_plane(t, h):
            nc.vector.tensor_tensor(pairs[h][:, 0, t, :], pairs[h][:, 0, t, :], pairs[h][:, 1, t, :], ALU.add)
            nc.vector.scalar_tensor_tensor(z2_planes[h][:, t, :], pairs[h][:, 0, t, :], gm15[:, t : t + 1],
                                           y[t][:, h * HALF : (h + 1) * HALF], ALU.mult, ALU.mult)

        def z_plane(t):
            nc.vector.tensor_scalar(z_planes[:, t, :], ds[t][:], gn_sb[:, t : t + 1], None, ALU.mult)

        for t in range(PACK):
            nc.vector.tensor_scalar(y[t][:], y_ps[t][:], 1.0, None, ALU.mult, ALU.max, accum_out=ends[:, t, 0:1])
            nc.vector.tensor_scalar(ds[t][:], y_ps[t][:], 1.0, None, ALU.mult, ALU.min, accum_out=ends[:, t, 1:2])
            pa = sbuf("pa%d" % t, [P, W], F32)
            old = sbuf("old%d" % t, [P, W], F32)
            ra = sbuf("ra%d" % t, [P, W], F32, tag="last_ra_then_pair" if t == PACK - 1 else None)
            nc.vector.tensor_tensor(biases[:, t, :], ends[:, t, :], rates[:, t, :], ALU.mult)
            if t in (0,1):
                nc.scalar.activation(old[:], y[t][:].indirect(n1_sb[:]), ACT.Copy)
            else:
                nc.vector.tensor_copy(old[:], y[t][:].indirect(n1_sb[:]))
            if t in ():
                nc.scalar.activation(pa[:], y[t][:].indirect(n2_sb[:]), ACT.Copy)
            else:
                nc.vector.tensor_copy(pa[:], y[t][:].indirect(n2_sb[:]))
            nc.vector.scalar_tensor_tensor(ra[:], old[:], 0.5, pa[:], ALU.mult, ALU.max)
            exp_pair(pairs[0], t, 0)
            if t in (3,):
                nc.vector.tensor_copy(ds[t][:].indirect(n1_sb[:]), ra[:])
            else:
                nc.scalar.activation(ds[t][:].indirect(n1_sb[:]), ra[:], ACT.Copy)
        pairs.append(sbuf("pair1", [P, 2, PACK, HALF], F32, tag="last_ra_then_pair"))
        for t in range(PACK):
            exp_pair(pairs[1], t, 1)

        def quantise(name, planes, words, scales, copy):
            grouped = sbuf(name, [P, HALF * PACK], BF16)
            interleave(copy, grouped, planes)
            nc.vector.quantize_mx(words.bitcast(FP8X4), scales, grouped[:])

        def z2_half(h):
            words = sbuf("z2_words%d" % h, [P, HALF], U32)
            scales = sbuf("z2_scales%d" % h, [P, HALF], U8)
            quantise("z2_grouped%d" % h, z2_planes[h][:], words[:], scales[:], nc.vector.tensor_copy)
            return words, scales

        def z_half(h):
            cols = slice(h * HALF, (h + 1) * HALF)
            words = sbuf("z_words%d" % h, [P, HALF], U32)
            scales = sbuf("z_scales%d" % h, [P, HALF], U8)
            quantise("z_grouped%d" % h, z_planes[:, :, cols], words[:], scales[:], nc.vector.tensor_copy)
            return words, scales

        hsb = [sbuf("h%d" % t, [P, S], F32) for t in range(PACK)]
        h_plain = [sbuf("h_plain%d" % t, [P, S], F32) for t in range(PACK)]
        sz = [sbuf("sz%d" % t, [P, S], F32) for t in range(PACK)]

        def second_product(h, operands):
            cols = slice(h * HALF, (h + 1) * HALF)
            banks = [psum.tile([P, HALF], F32, name="h_ps%d_%d" % (h, t), tag="bank%d" % (PACK * (1 - h) + t))
                     for t in range(PACK)]
            for i, (a, (words, scales)) in enumerate(operands):
                for t in range(PACK):
                    nc.tensor.matmul_mx(
                        banks[t][:],
                        lhsT=w23w[:, 2 * (N * a + P * t) : 2 * (N * a + P * (t + 1))].bitcast(FP4X4),
                        lhsT_scale=w23s[:, N * a + P * t : N * a + P * (t + 1)],
                        rhs=words[:].bitcast(FP8X4),
                        rhs_scale=scales[:],
                        start=(i == 0),
                        stop=(i == 1),
                    )
            return banks

        def negated_h(t, h, bank):
            cols = slice(h * HALF, (h + 1) * HALF)
            nc.scalar.activation(hsb[t][:, cols], bank[:], ACT.Copy, scale=-1.0)
            nc.sync.dma_start(h_plain[t][:, cols], hsb[t][:, cols])

        for t in range(PACK):
            z2_plane(t, 0)
        z2_first = z2_half(0)
        for t in range(PACK):
            z_plane(t)
        first_banks = second_product(0, ((1, z2_first), (0, z_half(0))))
        for t in range(PACK):
            negated_h(t, 0, first_banks[t])
        for t in range(PACK):
            nc.scalar.activation(sz[t][:, 0:HALF], first_banks[t][:], ACT.Abs)
        for t in range(PACK):
            z2_plane(t, 1)
        second_banks = second_product(1, ((0, z_half(1)), (1, z2_half(1))))

        for t in range(PACK):
            negated_h(t, 1, second_banks[t])

        out_rows = out_0.rearrange("(p t) c -> p t c", t=PACK)
        out_words = out_1[0].rearrange("p c r -> p (c r)").bitcast(I32)
        o_words = sbuf("o_words", [P, S], U32)
        o_scales = sbuf("o_scales", [P, S], U8)
        for h in range(2):
            cols = slice(h * HALF, (h + 1) * HALF)
            result = sbuf("result%d" % h, [P, PACK, HALF], F32)
            ea3 = sbuf("ea3_%d" % h, [P, PACK, HALF], F32)
            diff = sbuf("diff%d" % h, [P, PACK, HALF], F32)
            for t in range(PACK):
                if h == 0:
                    nc.scalar.activation(sz[t][:, HALF:S], second_banks[t][:], ACT.Abs)
                nc.scalar.activation(ea3[:, t, :], sz[t][:].indirect(list_half(n5_sb, h)), ACT.Exp, scale=neg_tau3[:, t : t + 1])
                nc.vector.tensor_tensor(diff[:, t, :], hsb[t][:].indirect(list_half(n6_sb, h)), h_plain[t][:, cols], ALU.subtract)
                if t % 2 == 1:
                    two = slice(t - 1, t + 1)
                    nc.vector.tensor_tensor(result[:, two, :], diff[:, two, :], ea3[:, two, :], ALU.mult)
                    nc.sync.dma_start(out_rows[:, two, cols], result[:, two, :])
            quantise("o_grouped%d" % h, result[:], o_words[:, cols], o_scales[:, cols],
                     nc.scalar.copy if h == 0 else nc.vector.tensor_copy)
            nc.sync.dma_start(out_words[:, cols], o_words[:, cols].bitcast(I32))
        for q in range(QUADS):
            queue = nc.sync if q % 2 == 0 else nc.scalar
            queue.dma_start(out_2[0, 4 * q : 4 * q + 4, :].bitcast(I32), o_scales[32 * q : 32 * q + 4, :].bitcast(I32))
